import numpy as np
import ml_dtypes


def mxq(x, axis, fmt="e4m3"):
    dtype, down = {"e4m3": (ml_dtypes.float8_e4m3fn, 7), "e5m2": (ml_dtypes.float8_e5m2, 14)}[fmt]
    v = np.moveaxis(np.asarray(x, np.float32).astype(ml_dtypes.bfloat16).astype(np.float64), axis, -1)
    blocks = v.reshape(v.shape[:-1] + (-1, 32))
    amax = np.abs(blocks).max(-1, keepdims=True)
    byte = np.maximum(np.where(amax > 0, np.frexp(amax)[1] - 1 + 127, 0) - down, 1)
    scale = np.exp2(byte - 127.0)
    codes = (blocks / scale).astype(np.float32).astype(dtype).astype(np.float64)
    return np.moveaxis((codes * scale).reshape(v.shape), -1, axis)


WIDE = False


def mx_kscale(k, group=512):
    if not WIDE:
        return np.ones(k)
    levels = np.array([18, -18])
    if group != 512:
        return np.exp2(np.random.permutation(np.resize(levels, k // group))).repeat(group)
    if k % 512:
        return np.exp2(np.random.permutation(np.resize(levels, k // 32))).repeat(32)
    a = np.empty((k // 512, 16))
    for p in range(k // 512):
        a[p, :8] = np.random.permutation(np.resize(levels, 8))
        for g in range(8):
            far = levels[np.abs(levels - a[p, g]) >= 10]
            a[p, g + 8] = far[np.random.randint(len(far))]
    return np.exp2(a.ravel()).repeat(32)


def f64(x):
    return np.asarray(x).astype(np.float64)


G, D, M, N = 4, 128, 256, 512


def setup_inputs():
    n = np.random.standard_normal
    s_d = mx_kscale(D, 0)
    return {
        "x": (n((G, D, M)) / s_d[:, None] / np.sqrt(D)).astype(np.float32),
        "c": (n((G, D, N)) * s_d[:, None]).astype(np.float32),
    }


def reference(x, c):
    xq = mxq(f64(x), 1, "e4m3")
    cq = mxq(f64(c), 1, "e4m3")
    z = xq.transpose(0, 2, 1) @ cq
    ss = np.sum(np.square(z), axis=-1, keepdims=True)
    y = z / np.sqrt(ss + 1e-06)
    return y

@@ -1,0 +1,140 @@
+from contextlib import ExitStack
+
+import concourse.mybir as mybir
+
+G, D, M, N = 4, 128, 256, 512
+FLOPS = 2 * G * D * M * N
+EPS = 1e-06
+
+F32 = mybir.dt.float32
+BF16 = mybir.dt.bfloat16
+U32 = mybir.dt.uint32
+U8 = mybir.dt.uint8
+FP8X4 = mybir.dt.float8_e4m3fn_x4
+ACT = mybir.ActivationFunctionType
+ALU = mybir.AluOpType
+
+P = 128
+PACK = 4
+ROWS = D // PACK
+M_TILE = 128
+HALF = N // 2
+RUN = 4
+C_VECTOR = 160
+X_VECTOR = 80
+
+
+def interleave(copy, grouped, raw, lo, hi):
+    copy(
+        out=grouped[:, lo:hi, :].rearrange("p (c i) j -> p c j i", i=RUN),
+        in_=raw[:, :, lo:hi].rearrange("p j (c i) -> p c j i", i=RUN),
+    )
+
+
+def quantize(nc, codes, scales, grouped, lo, hi):
+    nc.vector.quantize_mx(
+        out=codes[:, lo:hi].bitcast(FP8X4),
+        scales=scales[:, lo:hi],
+        in_=grouped[:, lo:hi, :].rearrange("p n j -> p (n j)"),
+    )
+
+
+def tile_rows_rows_kernel(tc, x, c, out):
+    nc = tc.nc
+    c_rows = c.rearrange("g (p j) n -> (g p) (j n)", j=PACK)
+    x_rows = x.rearrange("g (p j) m -> (g p) j m", j=PACK)
+    blocks = M // M_TILE
+    tiles = [(mb, g) for mb in range(blocks) for g in range(G)]
+
+    with ExitStack() as ctx:
+        sb = ctx.enter_context(tc.tile_pool(name="sb", bufs=1))
+        psum = ctx.enter_context(tc.psum_pool(name="psum", bufs=1))
+        ctx.enter_context(tc.manual_schedule())
+
+        c_raw = sb.tile([P, PACK * N], F32, name="c_raw")
+        first = (PACK - 1) * N + HALF
+        nc.sync.dma_start(out=c_raw[:, :first], in_=c_rows[:, :first])
+        nc.sync.dma_start(out=c_raw[:, first:], in_=c_rows[:, first:])
+        x_raw = []
+        for mb in range(blocks):
+            raw = sb.tile([P, PACK, M_TILE], F32, name="x_raw%d" % mb)
+            nc.sync.dma_start(out=raw[:], in_=x_rows[:, :, mb * M_TILE : (mb + 1) * M_TILE])
+            x_raw.append(raw)
+
+        one = sb.tile([P, 1], F32, name="one")
+        warm = sb.tile([P, 1], F32, name="warm")
+        nc.vector.memset(one[:], 1.0)
+        nc.scalar.activation(out=warm[:], in_=one[:], func=ACT.Abs_reciprocal_sqrt)
+
+        c_by_row = c_raw[:].rearrange("p (j n) -> p j n", j=PACK)
+        c_grouped = sb.tile([P, N, PACK], BF16, name="c_grouped", align_bytes=64)
+        c_codes = sb.tile([P, N], U32, name="c_codes", align_bytes=64)
+        c_scales = sb.tile([P, N], U8, name="c_scales", align_bytes=64)
+        for lo in (0, HALF):
+            interleave(nc.vector.tensor_copy, c_grouped, c_by_row, lo, lo + C_VECTOR)
+            interleave(nc.scalar.copy, c_grouped, c_by_row, lo + C_VECTOR, lo + HALF)
+        quantize(nc, c_codes, c_scales, c_grouped, 0, HALF)
+
+        x_grouped = [sb.tile([P, M_TILE, PACK], BF16, name="x_grouped%d" % mb, align_bytes=64) for mb in range(blocks)]
+        x_codes = [sb.tile([P, M_TILE], U32, name="x_codes%d" % mb, align_bytes=64) for mb in range(blocks)]
+        x_scales = [sb.tile([P, M_TILE], U8, name="x_scales%d" % mb, align_bytes=64) for mb in range(blocks)]
+        z = [psum.tile([M_TILE, N], F32, name="z%d" % t) for t in range(len(tiles))]
+
+        def multiply(mb):
+            for g in range(G):
+                rows = slice(g * ROWS, (g + 1) * ROWS)
+                nc.tensor.matmul_mx(
+                    out=z[mb * G + g][:],
+                    lhsT=x_codes[mb][rows, :].bitcast(FP8X4),
+                    lhsT_scale=x_scales[mb][rows, :],
+                    rhs=c_codes[rows, :].bitcast(FP8X4),
+                    rhs_scale=c_scales[rows, :],
+                    start=True,
+                    stop=True,
+                )
+
+        interleave(nc.vector.tensor_copy, x_grouped[0], x_raw[0], 0, X_VECTOR)
+        interleave(nc.scalar.copy, x_grouped[0], x_raw[0], X_VECTOR, M_TILE)
+        quantize(nc, c_codes, c_scales, c_grouped, HALF, N)
+        quantize(nc, x_codes[0], x_scales[0], x_grouped[0], 0, M_TILE)
+        multiply(0)
+        interleave(nc.vector.tensor_copy, x_grouped[1], x_raw[1], 0, M_TILE)
+        quantize(nc, x_codes[1], x_scales[1], x_grouped[1], 0, M_TILE)
+        multiply(1)
+
+        count = len(tiles)
+        ss = [sb.tile([P, 1], F32, name="ss%d" % t) for t in range(count)]
+        inv = [sb.tile([P, 1], F32, name="inv%d" % t) for t in range(count)]
+        y = [sb.tile([M_TILE, N], F32, name="y%d" % t) for t in range(count)]
+
+        def sum_squares(t):
+            squares = sb.tile([M_TILE, N], BF16, name="squares", bufs=2)
+            nc.scalar.activation(out=squares[:], in_=z[t][:], func=ACT.Square, accum_out=ss[t][:])
+
+        def mean_square(t):
+            stats = sb.tile([P, 6], F32, name="stats")
+            moments = sb.tile([P, 2], F32, name="moments")
+            nc.vector.bn_stats(out=stats[:], in_=z[t][:])
+            nc.vector.bn_aggr(out=moments[:], in_=stats[:])
+            nc.vector.tensor_scalar(
+                out=ss[t][:], in0=moments[:, 0:1], scalar1=moments[:, 0:1], scalar2=moments[:, 1:2],
+                op0=ALU.mult, op1=ALU.add,
+            )
+
+        def inverse_root(t, scale):
+            nc.scalar.activation(out=inv[t][:], in_=ss[t][:], func=ACT.Abs_reciprocal_sqrt, scale=scale, bias=EPS)
+
+        def scale_and_store(t):
+            mb, g = tiles[t]
+            nc.vector.tensor_scalar(out=y[t][:], in0=z[t][:], scalar1=inv[t][:], scalar2=None, op0=ALU.mult)
+            nc.sync.dma_start(out=out[g, mb * M_TILE : (mb + 1) * M_TILE, :], in_=y[t][:])
+
+        sum_squares(0)
+        mean_square(1)
+        inverse_root(0, 1.0)
+        scale_and_store(0)
+        for t in range(1, count):
+            if t + 1 < count:
+                sum_squares(t + 1)
+            inverse_root(t, float(N) if t == 1 else 1.0)
+            scale_and_store(t)

@@ -22,6 +22,7 @@ HALF = N // 2
 RUN = 4
 C_VECTOR = 160
 X_VECTOR = 80
+WARM_ROUNDS = 8
 
 
 def interleave(copy, grouped, raw, lo, hi):
@@ -66,6 +67,25 @@ def tile_rows_rows_kernel(tc, x, c, out):
         nc.vector.memset(one[:], 1.0)
         nc.scalar.activation(out=warm[:], in_=one[:], func=ACT.Abs_reciprocal_sqrt)
 
+        z = [psum.tile([M_TILE, N], F32, name="z%d" % t) for t in range(len(tiles))]
+        zeros = sb.tile([P, N, PACK], BF16, name="zeros", align_bytes=64)
+        warm_codes = sb.tile([P, N], U32, name="warm_codes", align_bytes=64)
+        warm_scales = sb.tile([P, N], U8, name="warm_scales", align_bytes=64)
+        nc.vector.memset(zeros[:].rearrange("p n j -> p (n j)").bitcast(U32), 0)
+        quantize(nc, warm_codes, warm_scales, zeros, 0, N)
+        for r in range(WARM_ROUNDS):
+            for g in range(G):
+                rows = slice(g * ROWS, (g + 1) * ROWS)
+                nc.tensor.matmul_mx(
+                    out=z[G + g][:],
+                    lhsT=warm_codes[rows, :M_TILE].bitcast(FP8X4),
+                    lhsT_scale=warm_scales[rows, :M_TILE],
+                    rhs=warm_codes[rows, :].bitcast(FP8X4),
+                    rhs_scale=warm_scales[rows, :],
+                    start=(r == 0),
+                    stop=(r == WARM_ROUNDS - 1),
+                )
+
         c_by_row = c_raw[:].rearrange("p (j n) -> p j n", j=PACK)
         c_grouped = sb.tile([P, N, PACK], BF16, name="c_grouped", align_bytes=64)
         c_codes = sb.tile([P, N], U32, name="c_codes", align_bytes=64)
@@ -78,7 +98,6 @@ def tile_rows_rows_kernel(tc, x, c, out):
         x_grouped = [sb.tile([P, M_TILE, PACK], BF16, name="x_grouped%d" % mb, align_bytes=64) for mb in range(blocks)]
         x_codes = [sb.tile([P, M_TILE], U32, name="x_codes%d" % mb, align_bytes=64) for mb in range(blocks)]
         x_scales = [sb.tile([P, M_TILE], U8, name="x_scales%d" % mb, align_bytes=64) for mb in range(blocks)]
-        z = [psum.tile([M_TILE, N], F32, name="z%d" % t) for t in range(len(tiles))]
 
         def multiply(mb):
             for g in range(G):

@@ -17,12 +17,14 @@ ALU = mybir.AluOpType
 P = 128
 PACK = 4
 ROWS = D // PACK
+PAIR = 2
+FIRST = ROWS
+SPAN = FIRST + PAIR * ROWS
 M_TILE = 128
-HALF = N // 2
+CHUNK = 128
+CHUNKS = N // CHUNK
 RUN = 4
-C_VECTOR = 160
-X_VECTOR = 80
-WARM_ROUNDS = 8
+LAST_VECTOR = 64
 
 
 def interleave(copy, grouped, raw, lo, hi):
@@ -32,96 +34,84 @@ def interleave(copy, grouped, raw, lo, hi):
     )
 
 
-def quantize(nc, codes, scales, grouped, lo, hi):
-    nc.vector.quantize_mx(
-        out=codes[:, lo:hi].bitcast(FP8X4),
-        scales=scales[:, lo:hi],
-        in_=grouped[:, lo:hi, :].rearrange("p n j -> p (n j)"),
-    )
-
-
 def tile_rows_rows_kernel(tc, x, c, out):
     nc = tc.nc
-    c_rows = c.rearrange("g (p j) n -> (g p) (j n)", j=PACK)
-    x_rows = x.rearrange("g (p j) m -> (g p) j m", j=PACK)
+    c_rows = c.rearrange("(h g) (p j) n -> h (g p) (j n)", g=PAIR, j=PACK)
+    x_rows = x.rearrange("(h g) (p j) m -> h (g p) j m", g=PAIR, j=PACK)
     blocks = M // M_TILE
-    tiles = [(mb, g) for mb in range(blocks) for g in range(G)]
+    tiles = [(h, mb, g) for h in range(G // PAIR) for mb in range(blocks) for g in range(PAIR)]
+    count = len(tiles)
 
     with ExitStack() as ctx:
         sb = ctx.enter_context(tc.tile_pool(name="sb", bufs=1))
         psum = ctx.enter_context(tc.psum_pool(name="psum", bufs=1))
         ctx.enter_context(tc.manual_schedule())
 
-        c_raw = sb.tile([P, PACK * N], F32, name="c_raw")
-        first = (PACK - 1) * N + HALF
-        nc.sync.dma_start(out=c_raw[:, :first], in_=c_rows[:, :first])
-        nc.sync.dma_start(out=c_raw[:, first:], in_=c_rows[:, first:])
-        x_raw = []
-        for mb in range(blocks):
-            raw = sb.tile([P, PACK, M_TILE], F32, name="x_raw%d" % mb)
-            nc.sync.dma_start(out=raw[:], in_=x_rows[:, :, mb * M_TILE : (mb + 1) * M_TILE])
-            x_raw.append(raw)
+        x_raw = sb.tile([SPAN, PACK, M], F32, name="x_raw")
+        c_raw = [sb.tile([SPAN, PACK * N], F32, name="c_raw%d" % h) for h in range(2)]
+        first = (PACK - 1) * N + N // 2
+        nc.sync.dma_start(out=x_raw[FIRST:, :, :], in_=x_rows[0])
+        nc.sync.dma_start(out=c_raw[0][FIRST:, :first], in_=c_rows[0][:, :first])
+        nc.sync.dma_start(out=c_raw[0][FIRST:, first:], in_=c_rows[0][:, first:])
+        nc.sync.dma_start(out=c_raw[1][FIRST:, :], in_=c_rows[1])
+        c_by_row = [raw[:].rearrange("p (j n) -> p j n", j=PACK) for raw in c_raw]
 
         one = sb.tile([P, 1], F32, name="one")
         warm = sb.tile([P, 1], F32, name="warm")
+        zeros = sb.tile([FIRST, CHUNK], F32, name="zeros")
+        nc.vector.memset(zeros[:], 0.0)
         nc.vector.memset(one[:], 1.0)
         nc.scalar.activation(out=warm[:], in_=one[:], func=ACT.Abs_reciprocal_sqrt)
 
-        z = [psum.tile([M_TILE, N], F32, name="z%d" % t) for t in range(len(tiles))]
-        zeros = sb.tile([P, N, PACK], BF16, name="zeros", align_bytes=64)
-        warm_codes = sb.tile([P, N], U32, name="warm_codes", align_bytes=64)
-        warm_scales = sb.tile([P, N], U8, name="warm_scales", align_bytes=64)
-        nc.vector.memset(zeros[:].rearrange("p n j -> p (n j)").bitcast(U32), 0)
-        quantize(nc, warm_codes, warm_scales, zeros, 0, N)
-        for r in range(WARM_ROUNDS):
-            for g in range(G):
-                rows = slice(g * ROWS, (g + 1) * ROWS)
+        def clear(copy, region):
+            width = region.shape[1]
+            copy(
+                out=region.rearrange("p (a b) -> p a b", b=CHUNK),
+                in_=zeros[:].unsqueeze(1).to_broadcast([FIRST, width // CHUNK, CHUNK]),
+            )
+
+        vector, scalar = nc.vector.tensor_copy, nc.scalar.copy
+        clear(vector, x_raw[:FIRST, :, :].rearrange("p j m -> p (j m)"))
+        clear(vector, c_raw[0][:FIRST, :])
+        clear(vector, c_raw[1][:FIRST, :N])
+        clear(scalar, c_raw[1][:FIRST, 2 * N :])
+
+        def operand(name, width):
+            return (
+                sb.tile([SPAN, width, PACK], BF16, name=name + "_grouped", align_bytes=64),
+                sb.tile([SPAN, width], U32, name=name + "_codes", align_bytes=64),
+                sb.tile([SPAN, width], U8, name=name + "_scales", align_bytes=64),
+            )
+
+        xs = [operand("x%d" % h, M) for h in range(2)]
+        cs = [operand("c%d" % h, N) for h in range(2)]
+
+        def quantize(op, k):
+            grouped, codes, scales = op
+            cols = slice(k * CHUNK, (k + 1) * CHUNK)
+            nc.vector.quantize_mx(
+                out=codes[:, cols].bitcast(FP8X4),
+                scales=scales[:, cols],
+                in_=grouped[:, cols, :].rearrange("p n j -> p (n j)"),
+            )
+
+        z = [psum.tile([M_TILE, N], F32, name="z%d" % t) for t in range(count)]
+
+        def multiply(h, mb, k):
+            cols = slice(k * CHUNK, (k + 1) * CHUNK)
+            m_cols = slice(mb * M_TILE, (mb + 1) * M_TILE)
+            for g in range(PAIR):
+                rows = slice(FIRST + g * ROWS, FIRST + (g + 1) * ROWS)
                 nc.tensor.matmul_mx(
-                    out=z[G + g][:],
-                    lhsT=warm_codes[rows, :M_TILE].bitcast(FP8X4),
-                    lhsT_scale=warm_scales[rows, :M_TILE],
-                    rhs=warm_codes[rows, :].bitcast(FP8X4),
-                    rhs_scale=warm_scales[rows, :],
-                    start=(r == 0),
-                    stop=(r == WARM_ROUNDS - 1),
-                )
-
-        c_by_row = c_raw[:].rearrange("p (j n) -> p j n", j=PACK)
-        c_grouped = sb.tile([P, N, PACK], BF16, name="c_grouped", align_bytes=64)
-        c_codes = sb.tile([P, N], U32, name="c_codes", align_bytes=64)
-        c_scales = sb.tile([P, N], U8, name="c_scales", align_bytes=64)
-        for lo in (0, HALF):
-            interleave(nc.vector.tensor_copy, c_grouped, c_by_row, lo, lo + C_VECTOR)
-            interleave(nc.scalar.copy, c_grouped, c_by_row, lo + C_VECTOR, lo + HALF)
-        quantize(nc, c_codes, c_scales, c_grouped, 0, HALF)
-
-        x_grouped = [sb.tile([P, M_TILE, PACK], BF16, name="x_grouped%d" % mb, align_bytes=64) for mb in range(blocks)]
-        x_codes = [sb.tile([P, M_TILE], U32, name="x_codes%d" % mb, align_bytes=64) for mb in range(blocks)]
-        x_scales = [sb.tile([P, M_TILE], U8, name="x_scales%d" % mb, align_bytes=64) for mb in range(blocks)]
-
-        def multiply(mb):
-            for g in range(G):
-                rows = slice(g * ROWS, (g + 1) * ROWS)
-                nc.tensor.matmul_mx(
-                    out=z[mb * G + g][:],
-                    lhsT=x_codes[mb][rows, :].bitcast(FP8X4),
-                    lhsT_scale=x_scales[mb][rows, :],
-                    rhs=c_codes[rows, :].bitcast(FP8X4),
-                    rhs_scale=c_scales[rows, :],
+                    out=z[tiles.index((h, mb, g))][:, cols],
+                    lhsT=xs[h][1][rows, m_cols].bitcast(FP8X4),
+                    lhsT_scale=xs[h][2][rows, m_cols],
+                    rhs=cs[h][1][rows, cols].bitcast(FP8X4),
+                    rhs_scale=cs[h][2][rows, cols],
                     start=True,
                     stop=True,
                 )
 
-        interleave(nc.vector.tensor_copy, x_grouped[0], x_raw[0], 0, X_VECTOR)
-        interleave(nc.scalar.copy, x_grouped[0], x_raw[0], X_VECTOR, M_TILE)
-        quantize(nc, c_codes, c_scales, c_grouped, HALF, N)
-        quantize(nc, x_codes[0], x_scales[0], x_grouped[0], 0, M_TILE)
-        multiply(0)
-        interleave(nc.vector.tensor_copy, x_grouped[1], x_raw[1], 0, M_TILE)
-        quantize(nc, x_codes[1], x_scales[1], x_grouped[1], 0, M_TILE)
-        multiply(1)
-
-        count = len(tiles)
         ss = [sb.tile([P, 1], F32, name="ss%d" % t) for t in range(count)]
         inv = [sb.tile([P, 1], F32, name="inv%d" % t) for t in range(count)]
         y = [sb.tile([M_TILE, N], F32, name="y%d" % t) for t in range(count)]
@@ -130,30 +120,61 @@ def tile_rows_rows_kernel(tc, x, c, out):
             squares = sb.tile([M_TILE, N], BF16, name="squares", bufs=2)
             nc.scalar.activation(out=squares[:], in_=z[t][:], func=ACT.Square, accum_out=ss[t][:])
 
-        def mean_square(t):
-            stats = sb.tile([P, 6], F32, name="stats")
-            moments = sb.tile([P, 2], F32, name="moments")
-            nc.vector.bn_stats(out=stats[:], in_=z[t][:])
-            nc.vector.bn_aggr(out=moments[:], in_=stats[:])
-            nc.vector.tensor_scalar(
-                out=ss[t][:], in0=moments[:, 0:1], scalar1=moments[:, 0:1], scalar2=moments[:, 1:2],
-                op0=ALU.mult, op1=ALU.add,
-            )
+        def inverse_root(t):
+            nc.scalar.activation(out=inv[t][:], in_=ss[t][:], func=ACT.Abs_reciprocal_sqrt, bias=EPS)
 
-        def inverse_root(t, scale):
-            nc.scalar.activation(out=inv[t][:], in_=ss[t][:], func=ACT.Abs_reciprocal_sqrt, scale=scale, bias=EPS)
+        def store(t):
+            h, mb, g = tiles[t]
+            nc.sync.dma_start(out=out[h * PAIR + g, mb * M_TILE : (mb + 1) * M_TILE, :], in_=y[t][:])
 
-        def scale_and_store(t):
-            mb, g = tiles[t]
+        def scale(t):
             nc.vector.tensor_scalar(out=y[t][:], in0=z[t][:], scalar1=inv[t][:], scalar2=None, op0=ALU.mult)
-            nc.sync.dma_start(out=out[g, mb * M_TILE : (mb + 1) * M_TILE, :], in_=y[t][:])
+            store(t)
+
+        def scale_on_scalar(t):
+            nc.scalar.activation(out=y[t][:], in_=z[t][:], func=ACT.Copy, scale=inv[t][:])
+            store(t)
+
+        def reload_x(mb):
+            cols = slice(mb * M_TILE, (mb + 1) * M_TILE)
+            nc.sync.dma_start(out=x_raw[FIRST:, :, cols], in_=x_rows[1][:, :, cols])
+
+        interleave(vector, xs[0][0], x_raw, 0, M_TILE)
+        reload_x(0)
+        clear(vector, c_raw[1][:FIRST, N : 2 * N])
+        quantize(xs[0], 0)
+
+        interleave(vector, cs[0][0], c_by_row[0], 0, CHUNK)
+        interleave(scalar, cs[0][0], c_by_row[0], CHUNK, 2 * CHUNK)
+        interleave(vector, cs[0][0], c_by_row[0], 2 * CHUNK, 3 * CHUNK + LAST_VECTOR)
+        interleave(scalar, cs[0][0], c_by_row[0], 3 * CHUNK + LAST_VECTOR, N)
+        for k in range(CHUNKS):
+            quantize(cs[0], k)
+            multiply(0, 0, k)
+
+        interleave(scalar, xs[0][0], x_raw, M_TILE, M)
+        reload_x(1)
+        interleave(vector, cs[1][0], c_by_row[1], 0, 2 * CHUNK)
+        interleave(scalar, cs[1][0], c_by_row[1], 3 * CHUNK, N)
+        quantize(xs[0], 1)
+        for k in range(CHUNKS):
+            multiply(0, 1, k)
+        interleave(vector, xs[1][0], x_raw, 0, M_TILE)
+        interleave(vector, cs[1][0], c_by_row[1], 2 * CHUNK, 3 * CHUNK)
+        quantize(xs[1], 0)
+        for k in range(CHUNKS):
+            quantize(cs[1], k)
+            multiply(1, 0, k)
+        interleave(vector, xs[1][0], x_raw, M_TILE, M)
 
         sum_squares(0)
-        mean_square(1)
-        inverse_root(0, 1.0)
-        scale_and_store(0)
-        for t in range(1, count):
-            if t + 1 < count:
-                sum_squares(t + 1)
-            inverse_root(t, float(N) if t == 1 else 1.0)
-            scale_and_store(t)
+        for t in range(count - 1):
+            sum_squares(t + 1)
+            inverse_root(t)
+            scale(t)
+            if t == 0:
+                quantize(xs[1], 1)
+                for k in range(CHUNKS):
+                    multiply(1, 1, k)
+        inverse_root(count - 1)
+        scale_on_scalar(count - 1)

@@ -22,14 +22,16 @@ FIRST = ROWS
 SPAN = FIRST + PAIR * ROWS
 M_TILE = 128
 CHUNK = 128
+HALF = N // 2
 CHUNKS = N // CHUNK
 RUN = 4
 LAST_VECTOR = 64
+NEXT_SCALAR = 224
 
 
-def interleave(copy, grouped, raw, lo, hi):
+def interleave(copy, grouped, raw, lo, hi, shift=0):
     copy(
-        out=grouped[:, lo:hi, :].rearrange("p (c i) j -> p c j i", i=RUN),
+        out=grouped[:, shift + lo : shift + hi, :].rearrange("p (c i) j -> p c j i", i=RUN),
         in_=raw[:, :, lo:hi].rearrange("p j (c i) -> p c j i", i=RUN),
     )
 
@@ -48,33 +50,38 @@ def tile_rows_rows_kernel(tc, x, c, out):
         ctx.enter_context(tc.manual_schedule())
 
         x_raw = sb.tile([SPAN, PACK, M], F32, name="x_raw")
-        c_raw = [sb.tile([SPAN, PACK * N], F32, name="c_raw%d" % h) for h in range(2)]
-        first = (PACK - 1) * N + N // 2
+        c_raw = sb.tile([SPAN, PACK * N], F32, name="c_raw")
+        c_next = sb.tile([SPAN, PACK, HALF], F32, name="c_next")
+        x_next = sb.tile([SPAN, PACK, M_TILE], F32, name="x_next")
+        c_by_row = c_raw[:].rearrange("p (j n) -> p j n", j=PACK)
+        c_second = c_rows[1].rearrange("p (j n) -> p j n", j=PACK)
+        first = (PACK - 1) * N + HALF
         nc.sync.dma_start(out=x_raw[FIRST:, :, :], in_=x_rows[0])
-        nc.sync.dma_start(out=c_raw[0][FIRST:, :first], in_=c_rows[0][:, :first])
-        nc.sync.dma_start(out=c_raw[0][FIRST:, first:], in_=c_rows[0][:, first:])
-        nc.sync.dma_start(out=c_raw[1][FIRST:, :], in_=c_rows[1])
-        c_by_row = [raw[:].rearrange("p (j n) -> p j n", j=PACK) for raw in c_raw]
+        nc.sync.dma_start(out=c_raw[FIRST:, :first], in_=c_rows[0][:, :first])
+        nc.sync.dma_start(out=c_raw[FIRST:, first:], in_=c_rows[0][:, first:])
+        nc.sync.dma_start(out=c_next[FIRST:, :, :], in_=c_second[:, :, :HALF])
+        nc.sync.dma_start(out=x_next[FIRST:, :, :], in_=x_rows[1][:, :, :M_TILE])
 
-        one = sb.tile([P, 1], F32, name="one")
-        warm = sb.tile([P, 1], F32, name="warm")
-        zeros = sb.tile([FIRST, CHUNK], F32, name="zeros")
-        nc.vector.memset(zeros[:], 0.0)
-        nc.vector.memset(one[:], 1.0)
-        nc.scalar.activation(out=warm[:], in_=one[:], func=ACT.Abs_reciprocal_sqrt)
+        flat = "p j n -> p (j n)"
+        x_flat = x_raw[:FIRST, :, :].rearrange(flat)
+        zeros = x_flat[:, :CHUNK]
+        nc.vector.memset(zeros.bitcast(U32), 0)
+        nc.vector.memset(x_flat[:, CHUNK : 4 * CHUNK].bitcast(U32), 0)
+        warm = sb.tile([FIRST, 1], F32, name="warm")
+        nc.scalar.activation(out=warm[:], in_=zeros[:, :1], func=ACT.Abs_reciprocal_sqrt, bias=EPS)
 
         def clear(copy, region):
             width = region.shape[1]
             copy(
                 out=region.rearrange("p (a b) -> p a b", b=CHUNK),
-                in_=zeros[:].unsqueeze(1).to_broadcast([FIRST, width // CHUNK, CHUNK]),
+                in_=zeros.unsqueeze(1).to_broadcast([FIRST, width // CHUNK, CHUNK]),
             )
 
         vector, scalar = nc.vector.tensor_copy, nc.scalar.copy
-        clear(vector, x_raw[:FIRST, :, :].rearrange("p j m -> p (j m)"))
-        clear(vector, c_raw[0][:FIRST, :])
-        clear(vector, c_raw[1][:FIRST, :N])
-        clear(scalar, c_raw[1][:FIRST, 2 * N :])
+        clear(vector, x_raw[:FIRST, 2:, :].rearrange(flat))
+        clear(vector, c_raw[:FIRST, :])
+        clear(vector, c_next[:FIRST, 0, :])
+        clear(scalar, x_next[:FIRST, :2, :].rearrange(flat))
 
         def operand(name, width):
             return (
@@ -95,7 +102,13 @@ def tile_rows_rows_kernel(tc, x, c, out):
                 in_=grouped[:, cols, :].rearrange("p n j -> p (n j)"),
             )
 
-        z = [psum.tile([M_TILE, N], F32, name="z%d" % t) for t in range(count)]
+        banks = [psum.tile([M_TILE, N], F32, name="bank%d" % t) for t in range(count)]
+        reused = tiles.index((1, 1, 0))
+
+        def z(t, cols):
+            if t == 0 and cols.start >= HALF:
+                return banks[0][:, cols]
+            return banks[reused if t == 0 else t][:, cols]
 
         def multiply(h, mb, k):
             cols = slice(k * CHUNK, (k + 1) * CHUNK)
@@ -103,7 +116,7 @@ def tile_rows_rows_kernel(tc, x, c, out):
             for g in range(PAIR):
                 rows = slice(FIRST + g * ROWS, FIRST + (g + 1) * ROWS)
                 nc.tensor.matmul_mx(
-                    out=z[tiles.index((h, mb, g))][:, cols],
+                    out=z(tiles.index((h, mb, g)), cols),
                     lhsT=xs[h][1][rows, m_cols].bitcast(FP8X4),
                     lhsT_scale=xs[h][2][rows, m_cols],
                     rhs=cs[h][1][rows, cols].bitcast(FP8X4),
@@ -118,7 +131,7 @@ def tile_rows_rows_kernel(tc, x, c, out):
 
         def sum_squares(t):
             squares = sb.tile([M_TILE, N], BF16, name="squares", bufs=2)
-            nc.scalar.activation(out=squares[:], in_=z[t][:], func=ACT.Square, accum_out=ss[t][:])
+            nc.scalar.activation(out=squares[:], in_=banks[t][:], func=ACT.Square, accum_out=ss[t][:])
 
         def inverse_root(t):
             nc.scalar.activation(out=inv[t][:], in_=ss[t][:], func=ACT.Abs_reciprocal_sqrt, bias=EPS)
@@ -128,53 +141,69 @@ def tile_rows_rows_kernel(tc, x, c, out):
             nc.sync.dma_start(out=out[h * PAIR + g, mb * M_TILE : (mb + 1) * M_TILE, :], in_=y[t][:])
 
         def scale(t):
-            nc.vector.tensor_scalar(out=y[t][:], in0=z[t][:], scalar1=inv[t][:], scalar2=None, op0=ALU.mult)
+            nc.vector.tensor_scalar(out=y[t][:], in0=banks[t][:], scalar1=inv[t][:], scalar2=None, op0=ALU.mult)
             store(t)
 
         def scale_on_scalar(t):
-            nc.scalar.activation(out=y[t][:], in_=z[t][:], func=ACT.Copy, scale=inv[t][:])
+            nc.scalar.activation(out=y[t][:], in_=banks[t][:], func=ACT.Copy, scale=inv[t][:])
             store(t)
 
-        def reload_x(mb):
-            cols = slice(mb * M_TILE, (mb + 1) * M_TILE)
-            nc.sync.dma_start(out=x_raw[FIRST:, :, cols], in_=x_rows[1][:, :, cols])
+        halves = [slice(0, HALF), slice(HALF, N)]
+        part = sb.tile([P, 1], F32, name="part")
+        part_eps = sb.tile([P, 1], F32, name="part_eps")
+
+        def half_squares(half, total):
+            squares = sb.tile([M_TILE, N], BF16, name="squares", bufs=2)
+            nc.scalar.activation(out=squares[:, :HALF], in_=z(0, halves[half]), func=ACT.Square, accum_out=total[:])
 
         interleave(vector, xs[0][0], x_raw, 0, M_TILE)
-        reload_x(0)
-        clear(vector, c_raw[1][:FIRST, N : 2 * N])
+        interleave(scalar, xs[0][0], x_raw, M_TILE, M)
+        nc.sync.dma_start(out=x_raw[FIRST:, :, :], in_=c_second[:, :, HALF:])
+        clear(vector, c_next[:FIRST, 1:, :].rearrange(flat))
+        clear(scalar, x_next[:FIRST, 2:, :].rearrange(flat))
         quantize(xs[0], 0)
+        quantize(xs[0], 1)
 
-        interleave(vector, cs[0][0], c_by_row[0], 0, CHUNK)
-        interleave(scalar, cs[0][0], c_by_row[0], CHUNK, 2 * CHUNK)
-        interleave(vector, cs[0][0], c_by_row[0], 2 * CHUNK, 3 * CHUNK + LAST_VECTOR)
-        interleave(scalar, cs[0][0], c_by_row[0], 3 * CHUNK + LAST_VECTOR, N)
+        interleave(vector, cs[0][0], c_by_row, 0, CHUNK)
+        nc.sync.dma_start(out=c_by_row[FIRST:, :, :M_TILE], in_=x_rows[1][:, :, M_TILE:])
+        interleave(scalar, cs[0][0], c_by_row, CHUNK, 2 * CHUNK)
+        interleave(vector, cs[0][0], c_by_row, 2 * CHUNK, 3 * CHUNK + LAST_VECTOR)
+        interleave(scalar, cs[0][0], c_by_row, 3 * CHUNK + LAST_VECTOR, N)
         for k in range(CHUNKS):
             quantize(cs[0], k)
             multiply(0, 0, k)
-
-        interleave(scalar, xs[0][0], x_raw, M_TILE, M)
-        reload_x(1)
-        interleave(vector, cs[1][0], c_by_row[1], 0, 2 * CHUNK)
-        interleave(scalar, cs[1][0], c_by_row[1], 3 * CHUNK, N)
-        quantize(xs[0], 1)
         for k in range(CHUNKS):
             multiply(0, 1, k)
-        interleave(vector, xs[1][0], x_raw, 0, M_TILE)
-        interleave(vector, cs[1][0], c_by_row[1], 2 * CHUNK, 3 * CHUNK)
+
+        interleave(scalar, cs[1][0], c_next, 0, CHUNK)
+        interleave(scalar, cs[1][0], c_next, CHUNK, NEXT_SCALAR)
+        interleave(vector, xs[1][0], x_next, 0, M_TILE)
+        interleave(vector, cs[1][0], c_next, NEXT_SCALAR, HALF)
+        quantize(cs[1], 0)
         quantize(xs[1], 0)
-        for k in range(CHUNKS):
+        multiply(1, 0, 0)
+        interleave(vector, cs[1][0], x_raw, 0, HALF, HALF)
+        quantize(cs[1], 1)
+        multiply(1, 0, 1)
+        interleave(vector, xs[1][0], c_by_row, 0, M_TILE, M_TILE)
+        for k in range(2, CHUNKS):
             quantize(cs[1], k)
             multiply(1, 0, k)
-        interleave(vector, xs[1][0], x_raw, M_TILE, M)
 
-        sum_squares(0)
-        for t in range(count - 1):
+        half_squares(0, part)
+        half_squares(1, ss[0])
+        nc.scalar.activation(out=part_eps[:], in_=part[:], func=ACT.Identity, bias=EPS)
+        sum_squares(1)
+        nc.scalar.activation(out=inv[0][:], in_=ss[0][:], func=ACT.Abs_reciprocal_sqrt, bias=part_eps[:])
+        for half in halves:
+            nc.vector.tensor_scalar(out=y[0][:, half], in0=z(0, half), scalar1=inv[0][:], scalar2=None, op0=ALU.mult)
+        store(0)
+        quantize(xs[1], 1)
+        for k in range(CHUNKS):
+            multiply(1, 1, k)
+        for t in range(1, count - 1):
             sum_squares(t + 1)
             inverse_root(t)
             scale(t)
-            if t == 0:
-                quantize(xs[1], 1)
-                for k in range(CHUNKS):
-                    multiply(1, 1, k)
         inverse_root(count - 1)
         scale_on_scalar(count - 1)

@@ -49,10 +49,10 @@ def tile_rows_rows_kernel(tc, x, c, out):
         psum = ctx.enter_context(tc.psum_pool(name="psum", bufs=1))
         ctx.enter_context(tc.manual_schedule())
 
-        x_raw = sb.tile([SPAN, PACK, M], F32, name="x_raw")
-        c_raw = sb.tile([SPAN, PACK * N], F32, name="c_raw")
-        c_next = sb.tile([SPAN, PACK, HALF], F32, name="c_next")
-        x_next = sb.tile([SPAN, PACK, M_TILE], F32, name="x_next")
+        x_raw = sb.tile([SPAN, PACK, M], F32, name="x_raw", align_bytes=256)
+        c_raw = sb.tile([SPAN, PACK * N], F32, name="c_raw", align_bytes=256)
+        c_next = sb.tile([SPAN, PACK, HALF], F32, name="c_next", align_bytes=256)
+        x_next = sb.tile([SPAN, PACK, M_TILE], F32, name="x_next", align_bytes=256)
         c_by_row = c_raw[:].rearrange("p (j n) -> p j n", j=PACK)
         c_second = c_rows[1].rearrange("p (j n) -> p j n", j=PACK)
         first = (PACK - 1) * N + HALF
@@ -127,7 +127,7 @@ def tile_rows_rows_kernel(tc, x, c, out):
 
         ss = [sb.tile([P, 1], F32, name="ss%d" % t) for t in range(count)]
         inv = [sb.tile([P, 1], F32, name="inv%d" % t) for t in range(count)]
-        y = [sb.tile([M_TILE, N], F32, name="y%d" % t) for t in range(count)]
+        y = [sb.tile([M_TILE, N], F32, name="y%d" % t, align_bytes=256) for t in range(count)]
 
         def sum_squares(t):
             squares = sb.tile([M_TILE, N], BF16, name="squares", bufs=2)

@@ -25,8 +25,7 @@ CHUNK = 128
 HALF = N // 2
 CHUNKS = N // CHUNK
 RUN = 4
-LAST_VECTOR = 64
-NEXT_SCALAR = 224
+NEXT_SCALAR = 192
 
 
 def interleave(copy, grouped, raw, lo, hi, shift=0):
@@ -38,7 +37,7 @@ def interleave(copy, grouped, raw, lo, hi, shift=0):
 
 def tile_rows_rows_kernel(tc, x, c, out):
     nc = tc.nc
-    c_rows = c.rearrange("(h g) (p j) n -> h (g p) (j n)", g=PAIR, j=PACK)
+    c_rows = c.rearrange("(h g) (p j) n -> h (g p) j n", g=PAIR, j=PACK)
     x_rows = x.rearrange("(h g) (p j) m -> h (g p) j m", g=PAIR, j=PACK)
     blocks = M // M_TILE
     tiles = [(h, mb, g) for h in range(G // PAIR) for mb in range(blocks) for g in range(PAIR)]
@@ -50,16 +49,13 @@ def tile_rows_rows_kernel(tc, x, c, out):
         ctx.enter_context(tc.manual_schedule())
 
         x_raw = sb.tile([SPAN, PACK, M], F32, name="x_raw", align_bytes=256)
-        c_raw = sb.tile([SPAN, PACK * N], F32, name="c_raw", align_bytes=256)
+        c_raw = [sb.tile([SPAN, PACK, HALF], F32, name="c_raw%d" % u, align_bytes=256) for u in range(2)]
         c_next = sb.tile([SPAN, PACK, HALF], F32, name="c_next", align_bytes=256)
         x_next = sb.tile([SPAN, PACK, M_TILE], F32, name="x_next", align_bytes=256)
-        c_by_row = c_raw[:].rearrange("p (j n) -> p j n", j=PACK)
-        c_second = c_rows[1].rearrange("p (j n) -> p j n", j=PACK)
-        first = (PACK - 1) * N + HALF
         nc.sync.dma_start(out=x_raw[FIRST:, :, :], in_=x_rows[0])
-        nc.sync.dma_start(out=c_raw[FIRST:, :first], in_=c_rows[0][:, :first])
-        nc.sync.dma_start(out=c_raw[FIRST:, first:], in_=c_rows[0][:, first:])
-        nc.sync.dma_start(out=c_next[FIRST:, :, :], in_=c_second[:, :, :HALF])
+        nc.sync.dma_start(out=c_raw[0][FIRST:, :, :], in_=c_rows[0][:, :, :HALF])
+        nc.sync.dma_start(out=c_raw[1][FIRST:, :, :], in_=c_rows[0][:, :, HALF:])
+        nc.sync.dma_start(out=c_next[FIRST:, :, :], in_=c_rows[1][:, :, :HALF])
         nc.sync.dma_start(out=x_next[FIRST:, :, :], in_=x_rows[1][:, :, :M_TILE])
 
         flat = "p j n -> p (j n)"
@@ -79,8 +75,9 @@ def tile_rows_rows_kernel(tc, x, c, out):
 
         vector, scalar = nc.vector.tensor_copy, nc.scalar.copy
         clear(vector, x_raw[:FIRST, 2:, :].rearrange(flat))
-        clear(vector, c_raw[:FIRST, :])
-        clear(vector, c_next[:FIRST, 0, :])
+        clear(vector, c_raw[0][:FIRST, :, :].rearrange(flat))
+        clear(vector, c_raw[1][:FIRST, :, :].rearrange(flat))
+        clear(vector, c_next[:FIRST, :2, :].rearrange(flat))
         clear(scalar, x_next[:FIRST, :2, :].rearrange(flat))
 
         def operand(name, width):
@@ -144,10 +141,6 @@ def tile_rows_rows_kernel(tc, x, c, out):
             nc.vector.tensor_scalar(out=y[t][:], in0=banks[t][:], scalar1=inv[t][:], scalar2=None, op0=ALU.mult)
             store(t)
 
-        def scale_on_scalar(t):
-            nc.scalar.activation(out=y[t][:], in_=banks[t][:], func=ACT.Copy, scale=inv[t][:])
-            store(t)
-
         halves = [slice(0, HALF), slice(HALF, N)]
         part = sb.tile([P, 1], F32, name="part")
         part_eps = sb.tile([P, 1], F32, name="part_eps")
@@ -158,17 +151,17 @@ def tile_rows_rows_kernel(tc, x, c, out):
 
         interleave(vector, xs[0][0], x_raw, 0, M_TILE)
         interleave(scalar, xs[0][0], x_raw, M_TILE, M)
-        nc.sync.dma_start(out=x_raw[FIRST:, :, :], in_=c_second[:, :, HALF:])
-        clear(vector, c_next[:FIRST, 1:, :].rearrange(flat))
-        clear(scalar, x_next[:FIRST, 2:, :].rearrange(flat))
+        nc.sync.dma_start(out=x_raw[FIRST:, :, :], in_=c_rows[1][:, :, HALF:])
+        clear(vector, c_next[:FIRST, 2:, :].rearrange(flat))
+        clear(vector, x_next[:FIRST, 2:, :].rearrange(flat))
+
+        interleave(vector, cs[0][0], c_raw[0], 0, CHUNK)
+        nc.sync.dma_start(out=c_raw[0][FIRST:, :, :M_TILE], in_=x_rows[1][:, :, M_TILE:])
+        interleave(scalar, cs[0][0], c_raw[0], CHUNK, HALF)
         quantize(xs[0], 0)
         quantize(xs[0], 1)
-
-        interleave(vector, cs[0][0], c_by_row, 0, CHUNK)
-        nc.sync.dma_start(out=c_by_row[FIRST:, :, :M_TILE], in_=x_rows[1][:, :, M_TILE:])
-        interleave(scalar, cs[0][0], c_by_row, CHUNK, 2 * CHUNK)
-        interleave(vector, cs[0][0], c_by_row, 2 * CHUNK, 3 * CHUNK + LAST_VECTOR)
-        interleave(scalar, cs[0][0], c_by_row, 3 * CHUNK + LAST_VECTOR, N)
+        interleave(vector, cs[0][0], c_raw[1], 0, CHUNK, HALF)
+        interleave(scalar, cs[0][0], c_raw[1], CHUNK, HALF, HALF)
         for k in range(CHUNKS):
             quantize(cs[0], k)
             multiply(0, 0, k)
@@ -185,7 +178,7 @@ def tile_rows_rows_kernel(tc, x, c, out):
         interleave(vector, cs[1][0], x_raw, 0, HALF, HALF)
         quantize(cs[1], 1)
         multiply(1, 0, 1)
-        interleave(vector, xs[1][0], c_by_row, 0, M_TILE, M_TILE)
+        interleave(vector, xs[1][0], c_raw[0], 0, M_TILE, M_TILE)
         for k in range(2, CHUNKS):
             quantize(cs[1], k)
             multiply(1, 0, k)
@@ -201,9 +194,12 @@ def tile_rows_rows_kernel(tc, x, c, out):
         quantize(xs[1], 1)
         for k in range(CHUNKS):
             multiply(1, 1, k)
-        for t in range(1, count - 1):
+        for t in range(1, count - 2):
             sum_squares(t + 1)
             inverse_root(t)
             scale(t)
+        inverse_root(count - 2)
+        scale(count - 2)
+        sum_squares(count - 1)
         inverse_root(count - 1)
-        scale_on_scalar(count - 1)
+        scale(count - 1)

@@ -30,8 +30,8 @@ NEXT_SCALAR = 192
 
 def interleave(copy, grouped, raw, lo, hi, shift=0):
     copy(
-        out=grouped[:, shift + lo : shift + hi, :].rearrange("p (c i) j -> p c j i", i=RUN),
-        in_=raw[:, :, lo:hi].rearrange("p j (c i) -> p c j i", i=RUN),
+        out=grouped[:, shift + lo : shift + hi, :].rearrange("p (c a i) j -> p a c j i", a=2, i=RUN),
+        in_=raw[:, :, lo:hi].rearrange("p j (c a i) -> p a c j i", a=2, i=RUN),
     )
 
 

@@ -26,6 +26,7 @@ HALF = N // 2
 CHUNKS = N // CHUNK
 RUN = 4
 NEXT_SCALAR = 192
+X_VECTOR = 168
 
 
 def interleave(copy, grouped, raw, lo, hi, shift=0):
@@ -77,8 +78,8 @@ def tile_rows_rows_kernel(tc, x, c, out):
         clear(vector, x_raw[:FIRST, 2:, :].rearrange(flat))
         clear(vector, c_raw[0][:FIRST, :, :].rearrange(flat))
         clear(vector, c_raw[1][:FIRST, :, :].rearrange(flat))
-        clear(vector, c_next[:FIRST, :2, :].rearrange(flat))
-        clear(scalar, x_next[:FIRST, :2, :].rearrange(flat))
+        clear(vector, c_next[:FIRST, :3, :].rearrange(flat))
+        clear(scalar, x_next[:FIRST, :, :].rearrange(flat))
 
         def operand(name, width):
             return (
@@ -150,10 +151,10 @@ def tile_rows_rows_kernel(tc, x, c, out):
             nc.scalar.activation(out=squares[:, :HALF], in_=z(0, halves[half]), func=ACT.Square, accum_out=total[:])
 
         interleave(vector, xs[0][0], x_raw, 0, M_TILE)
-        interleave(scalar, xs[0][0], x_raw, M_TILE, M)
+        interleave(vector, xs[0][0], x_raw, M_TILE, X_VECTOR)
+        interleave(scalar, xs[0][0], x_raw, X_VECTOR, M)
         nc.sync.dma_start(out=x_raw[FIRST:, :, :], in_=c_rows[1][:, :, HALF:])
-        clear(vector, c_next[:FIRST, 2:, :].rearrange(flat))
-        clear(vector, x_next[:FIRST, 2:, :].rearrange(flat))
+        clear(vector, c_next[:FIRST, 3:, :].rearrange(flat))
 
         interleave(vector, cs[0][0], c_raw[0], 0, CHUNK)
         nc.sync.dma_start(out=c_raw[0][FIRST:, :, :M_TILE], in_=x_rows[1][:, :, M_TILE:])

@@ -59,27 +59,24 @@ def tile_rows_rows_kernel(tc, x, c, out):
         nc.sync.dma_start(out=c_next[FIRST:, :, :], in_=c_rows[1][:, :, :HALF])
         nc.sync.dma_start(out=x_next[FIRST:, :, :], in_=x_rows[1][:, :, :M_TILE])
 
-        flat = "p j n -> p (j n)"
-        x_flat = x_raw[:FIRST, :, :].rearrange(flat)
-        zeros = x_flat[:, :CHUNK]
-        nc.vector.memset(zeros.bitcast(U32), 0)
-        nc.vector.memset(x_flat[:, CHUNK : 4 * CHUNK].bitcast(U32), 0)
-        warm = sb.tile([FIRST, 1], F32, name="warm")
-        nc.scalar.activation(out=warm[:], in_=zeros[:, :1], func=ACT.Abs_reciprocal_sqrt, bias=EPS)
-
-        def clear(copy, region):
-            width = region.shape[1]
-            copy(
-                out=region.rearrange("p (a b) -> p a b", b=CHUNK),
-                in_=zeros.unsqueeze(1).to_broadcast([FIRST, width // CHUNK, CHUNK]),
-            )
+        def clear(copy, region, zeros):
+            rows, width = region.shape[1:]
+            copy(out=region, in_=zeros[:FIRST, :1, :width].to_broadcast([FIRST, rows, width]))
 
         vector, scalar = nc.vector.tensor_copy, nc.scalar.copy
-        clear(vector, x_raw[:FIRST, 2:, :].rearrange(flat))
-        clear(vector, c_raw[0][:FIRST, :, :].rearrange(flat))
-        clear(vector, c_raw[1][:FIRST, :, :].rearrange(flat))
-        clear(vector, c_next[:FIRST, :3, :].rearrange(flat))
-        clear(scalar, x_next[:FIRST, :, :].rearrange(flat))
+        x_chunks = x_raw[:FIRST, :, :].rearrange("p j (a b) -> p (j a) b", b=CHUNK)
+        nc.vector.memset(x_chunks[:, 0, :].bitcast(U32), 0)
+        nc.vector.memset(x_chunks[:, 1:PACK, :].bitcast(U32), 0)
+        clear(vector, x_chunks[:, PACK:, :], x_raw)
+        clear(vector, c_raw[0][:FIRST, :, CHUNK:], x_raw)
+        clear(vector, c_raw[1][:FIRST, :, CHUNK:], x_raw)
+        clear(vector, c_next[:FIRST, :, :NEXT_SCALAR], x_raw)
+        warm = sb.tile([FIRST, 1], F32, name="warm")
+        nc.scalar.activation(out=warm[:], in_=c_raw[1][:FIRST, 0, CHUNK : CHUNK + 1], func=ACT.Abs_reciprocal_sqrt, bias=EPS)
+        clear(scalar, x_next[:FIRST, :2, :], x_raw)
+        clear(scalar, x_next[:FIRST, 2:, :], c_next)
+        clear(vector, c_raw[0][:FIRST, :, :CHUNK], x_raw)
+        clear(vector, c_raw[1][:FIRST, :, :CHUNK], c_next)
 
         def operand(name, width):
             return (
@@ -150,11 +147,10 @@ def tile_rows_rows_kernel(tc, x, c, out):
             squares = sb.tile([M_TILE, N], BF16, name="squares", bufs=2)
             nc.scalar.activation(out=squares[:, :HALF], in_=z(0, halves[half]), func=ACT.Square, accum_out=total[:])
 
-        interleave(vector, xs[0][0], x_raw, 0, M_TILE)
-        interleave(vector, xs[0][0], x_raw, M_TILE, X_VECTOR)
+        interleave(vector, xs[0][0], x_raw, 0, X_VECTOR)
         interleave(scalar, xs[0][0], x_raw, X_VECTOR, M)
         nc.sync.dma_start(out=x_raw[FIRST:, :, :], in_=c_rows[1][:, :, HALF:])
-        clear(vector, c_next[:FIRST, 3:, :].rearrange(flat))
+        clear(vector, c_next[:FIRST, :, NEXT_SCALAR:], c_raw[0])
 
         interleave(vector, cs[0][0], c_raw[0], 0, CHUNK)
         nc.sync.dma_start(out=c_raw[0][FIRST:, :, :M_TILE], in_=x_rows[1][:, :, M_TILE:])

@@ -25,7 +25,7 @@ CHUNK = 128
 HALF = N // 2
 CHUNKS = N // CHUNK
 RUN = 4
-NEXT_SCALAR = 192
+NEXT_SCALAR = 208
 X_VECTOR = 168
 
 

from contextlib import ExitStack

import concourse.mybir as mybir

G, D, M, N = 4, 128, 256, 512
FLOPS = 2 * G * D * M * N
EPS = 1e-06

F32 = mybir.dt.float32
BF16 = mybir.dt.bfloat16
U32 = mybir.dt.uint32
U8 = mybir.dt.uint8
FP8X4 = mybir.dt.float8_e4m3fn_x4
ACT = mybir.ActivationFunctionType
ALU = mybir.AluOpType

P = 128
PACK = 4
ROWS = D // PACK
PAIR = 2
FIRST = ROWS
SPAN = FIRST + PAIR * ROWS
M_TILE = 128
CHUNK = 128
HALF = N // 2
CHUNKS = N // CHUNK
RUN = 4
NEXT_SCALAR = 208
X_VECTOR = 168


def interleave(copy, grouped, raw, lo, hi, shift=0):
    copy(
        out=grouped[:, shift + lo : shift + hi, :].rearrange("p (c a i) j -> p a c j i", a=2, i=RUN),
        in_=raw[:, :, lo:hi].rearrange("p j (c a i) -> p a c j i", a=2, i=RUN),
    )


def tile_rows_rows_kernel(tc, x, c, out):
    nc = tc.nc
    c_rows = c.rearrange("(h g) (p j) n -> h (g p) j n", g=PAIR, j=PACK)
    x_rows = x.rearrange("(h g) (p j) m -> h (g p) j m", g=PAIR, j=PACK)
    blocks = M // M_TILE
    tiles = [(h, mb, g) for h in range(G // PAIR) for mb in range(blocks) for g in range(PAIR)]
    count = len(tiles)

    with ExitStack() as ctx:
        sb = ctx.enter_context(tc.tile_pool(name="sb", bufs=1))
        psum = ctx.enter_context(tc.psum_pool(name="psum", bufs=1))
        ctx.enter_context(tc.manual_schedule())

        x_raw = sb.tile([SPAN, PACK, M], F32, name="x_raw", align_bytes=256)
        c_raw = [sb.tile([SPAN, PACK, HALF], F32, name="c_raw%d" % u, align_bytes=256) for u in range(2)]
        c_next = sb.tile([SPAN, PACK, HALF], F32, name="c_next", align_bytes=256)
        x_next = sb.tile([SPAN, PACK, M_TILE], F32, name="x_next", align_bytes=256)
        nc.sync.dma_start(out=x_raw[FIRST:, :, :], in_=x_rows[0])
        nc.sync.dma_start(out=c_raw[0][FIRST:, :, :], in_=c_rows[0][:, :, :HALF])
        nc.sync.dma_start(out=c_raw[1][FIRST:, :, :], in_=c_rows[0][:, :, HALF:])
        nc.sync.dma_start(out=c_next[FIRST:, :, :], in_=c_rows[1][:, :, :HALF])
        nc.sync.dma_start(out=x_next[FIRST:, :, :], in_=x_rows[1][:, :, :M_TILE])

        def clear(copy, region, zeros):
            rows, width = region.shape[1:]
            copy(out=region, in_=zeros[:FIRST, :1, :width].to_broadcast([FIRST, rows, width]))

        vector, scalar = nc.vector.tensor_copy, nc.scalar.copy
        x_chunks = x_raw[:FIRST, :, :].rearrange("p j (a b) -> p (j a) b", b=CHUNK)
        nc.vector.memset(x_chunks[:, 0, :].bitcast(U32), 0)
        nc.vector.memset(x_chunks[:, 1:PACK, :].bitcast(U32), 0)
        clear(vector, x_chunks[:, PACK:, :], x_raw)
        clear(vector, c_raw[0][:FIRST, :, CHUNK:], x_raw)
        clear(vector, c_raw[1][:FIRST, :, CHUNK:], x_raw)
        clear(vector, c_next[:FIRST, :, :NEXT_SCALAR], x_raw)
        warm = sb.tile([FIRST, 1], F32, name="warm")
        nc.scalar.activation(out=warm[:], in_=c_raw[1][:FIRST, 0, CHUNK : CHUNK + 1], func=ACT.Abs_reciprocal_sqrt, bias=EPS)
        clear(scalar, x_next[:FIRST, :2, :], x_raw)
        clear(scalar, x_next[:FIRST, 2:, :], c_next)
        clear(vector, c_raw[0][:FIRST, :, :CHUNK], x_raw)
        clear(vector, c_raw[1][:FIRST, :, :CHUNK], c_next)

        def operand(name, width):
            return (
                sb.tile([SPAN, width, PACK], BF16, name=name + "_grouped", align_bytes=64),
                sb.tile([SPAN, width], U32, name=name + "_codes", align_bytes=64),
                sb.tile([SPAN, width], U8, name=name + "_scales", align_bytes=64),
            )

        xs = [operand("x%d" % h, M) for h in range(2)]
        cs = [operand("c%d" % h, N) for h in range(2)]

        def quantize(op, k):
            grouped, codes, scales = op
            cols = slice(k * CHUNK, (k + 1) * CHUNK)
            nc.vector.quantize_mx(
                out=codes[:, cols].bitcast(FP8X4),
                scales=scales[:, cols],
                in_=grouped[:, cols, :].rearrange("p n j -> p (n j)"),
            )

        banks = [psum.tile([M_TILE, N], F32, name="bank%d" % t) for t in range(count)]
        reused = tiles.index((1, 1, 0))

        def z(t, cols):
            if t == 0 and cols.start >= HALF:
                return banks[0][:, cols]
            return banks[reused if t == 0 else t][:, cols]

        def multiply(h, mb, k):
            cols = slice(k * CHUNK, (k + 1) * CHUNK)
            m_cols = slice(mb * M_TILE, (mb + 1) * M_TILE)
            for g in range(PAIR):
                rows = slice(FIRST + g * ROWS, FIRST + (g + 1) * ROWS)
                nc.tensor.matmul_mx(
                    out=z(tiles.index((h, mb, g)), cols),
                    lhsT=xs[h][1][rows, m_cols].bitcast(FP8X4),
                    lhsT_scale=xs[h][2][rows, m_cols],
                    rhs=cs[h][1][rows, cols].bitcast(FP8X4),
                    rhs_scale=cs[h][2][rows, cols],
                    start=True,
                    stop=True,
                )

        ss = [sb.tile([P, 1], F32, name="ss%d" % t) for t in range(count)]
        inv = [sb.tile([P, 1], F32, name="inv%d" % t) for t in range(count)]
        y = [sb.tile([M_TILE, N], F32, name="y%d" % t, align_bytes=256) for t in range(count)]

        def sum_squares(t):
            squares = sb.tile([M_TILE, N], BF16, name="squares", bufs=2)
            nc.scalar.activation(out=squares[:], in_=banks[t][:], func=ACT.Square, accum_out=ss[t][:])

        def inverse_root(t):
            nc.scalar.activation(out=inv[t][:], in_=ss[t][:], func=ACT.Abs_reciprocal_sqrt, bias=EPS)

        def store(t):
            h, mb, g = tiles[t]
            nc.sync.dma_start(out=out[h * PAIR + g, mb * M_TILE : (mb + 1) * M_TILE, :], in_=y[t][:])

        def scale(t):
            nc.vector.tensor_scalar(out=y[t][:], in0=banks[t][:], scalar1=inv[t][:], scalar2=None, op0=ALU.mult)
            store(t)

        halves = [slice(0, HALF), slice(HALF, N)]
        part = sb.tile([P, 1], F32, name="part")
        part_eps = sb.tile([P, 1], F32, name="part_eps")

        def half_squares(half, total):
            squares = sb.tile([M_TILE, N], BF16, name="squares", bufs=2)
            nc.scalar.activation(out=squares[:, :HALF], in_=z(0, halves[half]), func=ACT.Square, accum_out=total[:])

        interleave(vector, xs[0][0], x_raw, 0, X_VECTOR)
        interleave(scalar, xs[0][0], x_raw, X_VECTOR, M)
        nc.sync.dma_start(out=x_raw[FIRST:, :, :], in_=c_rows[1][:, :, HALF:])
        clear(vector, c_next[:FIRST, :, NEXT_SCALAR:], c_raw[0])

        interleave(vector, cs[0][0], c_raw[0], 0, CHUNK)
        nc.sync.dma_start(out=c_raw[0][FIRST:, :, :M_TILE], in_=x_rows[1][:, :, M_TILE:])
        interleave(scalar, cs[0][0], c_raw[0], CHUNK, HALF)
        quantize(xs[0], 0)
        quantize(xs[0], 1)
        interleave(vector, cs[0][0], c_raw[1], 0, CHUNK, HALF)
        interleave(scalar, cs[0][0], c_raw[1], CHUNK, HALF, HALF)
        for k in range(CHUNKS):
            quantize(cs[0], k)
            multiply(0, 0, k)
        for k in range(CHUNKS):
            multiply(0, 1, k)

        interleave(scalar, cs[1][0], c_next, 0, CHUNK)
        interleave(scalar, cs[1][0], c_next, CHUNK, NEXT_SCALAR)
        interleave(vector, xs[1][0], x_next, 0, M_TILE)
        interleave(vector, cs[1][0], c_next, NEXT_SCALAR, HALF)
        quantize(cs[1], 0)
        quantize(xs[1], 0)
        multiply(1, 0, 0)
        interleave(vector, cs[1][0], x_raw, 0, HALF, HALF)
        quantize(cs[1], 1)
        multiply(1, 0, 1)
        interleave(vector, xs[1][0], c_raw[0], 0, M_TILE, M_TILE)
        for k in range(2, CHUNKS):
            quantize(cs[1], k)
            multiply(1, 0, k)

        half_squares(0, part)
        half_squares(1, ss[0])
        nc.scalar.activation(out=part_eps[:], in_=part[:], func=ACT.Identity, bias=EPS)
        sum_squares(1)
        nc.scalar.activation(out=inv[0][:], in_=ss[0][:], func=ACT.Abs_reciprocal_sqrt, bias=part_eps[:])
        for half in halves:
            nc.vector.tensor_scalar(out=y[0][:, half], in0=z(0, half), scalar1=inv[0][:], scalar2=None, op0=ALU.mult)
        store(0)
        quantize(xs[1], 1)
        for k in range(CHUNKS):
            multiply(1, 1, k)
        for t in range(1, count - 2):
            sum_squares(t + 1)
            inverse_root(t)
            scale(t)
        inverse_root(count - 2)
        scale(count - 2)
        sum_squares(count - 1)
        inverse_root(count - 1)
        scale(count - 1)
